import numpy as np
import ml_dtypes


def mxq(x, axis, fmt="e4m3"):
    dtype, down = {"e4m3": (ml_dtypes.float8_e4m3fn, 7), "e5m2": (ml_dtypes.float8_e5m2, 14)}[fmt]
    v = np.moveaxis(np.asarray(x, np.float32).astype(ml_dtypes.bfloat16).astype(np.float64), axis, -1)
    blocks = v.reshape(v.shape[:-1] + (-1, 32))
    amax = np.abs(blocks).max(-1, keepdims=True)
    byte = np.maximum(np.where(amax > 0, np.frexp(amax)[1] - 1 + 127, 0) - down, 1)
    scale = np.exp2(byte - 127.0)
    codes = (blocks / scale).astype(np.float32).astype(dtype).astype(np.float64)
    return np.moveaxis((codes * scale).reshape(v.shape), -1, axis)


WIDE = False


def mx_kscale(k):
    if not WIDE:
        return np.ones(k)
    levels = np.array([10, -10, 5, -5, 0])
    if k % 512:
        return np.exp2(np.random.permutation(np.resize(levels, k // 32))).repeat(32)
    a = np.empty((k // 512, 16))
    for p in range(k // 512):
        a[p, :8] = np.random.permutation(np.resize(levels, 8))
        for g in range(8):
            far = levels[np.abs(levels - a[p, g]) >= 10]
            a[p, g + 8] = far[np.random.randint(len(far))]
    return np.exp2(a.ravel()).repeat(32)


def f64(x):
    return np.asarray(x).astype(np.float64)


def striped(idx):
    return np.tile(idx.reshape(-1, 16).T, (8, 1)).astype(np.uint16)


def unstriped(offs):
    return offs[:16].T.reshape(-1).astype(np.int64)


E2M1 = np.array([0.0, 0.5, 1.0, 1.5, 2.0, 3.0, 4.0, 6.0, -0.0, -0.5, -1.0, -1.5, -2.0, -3.0, -4.0, -6.0])


def pack_weight(w, fmt):
    k, n = w.shape
    w = f64(np.asarray(w, np.float32).astype(ml_dtypes.bfloat16)).reshape(k // 32, 32, n)
    amax = np.abs(w).max(1)
    if fmt == "e4m3":
        byte = np.frexp(amax)[1] - 1 + 127 - 7
    else:
        mant, ex = np.frexp(amax / 6.0)
        byte = np.where(mant > 0.5, ex, ex - 1) + 127
    byte = np.clip(np.where(amax > 0, byte, 1), 1, 254)
    scaled = (w * np.exp2(127.0 - byte)[:, None, :]).reshape(k, n).astype(np.float32)
    by_word = np.ascontiguousarray(scaled.reshape(k // 512, 128, 4, n).transpose(0, 1, 3, 2))
    if fmt == "e4m3":
        words = by_word.astype(ml_dtypes.float8_e4m3fn).view(np.uint8)
    else:
        c = by_word.astype(ml_dtypes.float4_e2m1fn).view(np.uint8) & 0xF
        words = (c[..., 0::2] | (c[..., 1::2] << 4)).reshape(k // 512, 128, 2 * n)
    return np.ascontiguousarray(words), np.ascontiguousarray(byte.astype(np.uint8).reshape(k // 512, 16, n))


def unpack_weight(words, scales, fmt):
    g, _, n = scales.shape
    words = np.ascontiguousarray(words).reshape(g, 128, n, -1)
    if fmt == "e4m3":
        vals = words.view(ml_dtypes.float8_e4m3fn).astype(np.float64)
    else:
        nib = np.empty((g, 128, n, 4), np.uint8)
        nib[..., 0::2] = words & 0xF
        nib[..., 1::2] = words >> 4
        vals = E2M1[nib]
    vals = vals * np.repeat(np.exp2(scales.astype(np.float64) - 127.0), 8, axis=1)[..., None]
    return vals.transpose(0, 1, 3, 2).reshape(g * 512, n)


def gelu(v):
    return 0.5 * v * (1.0 + np.tanh(np.sqrt(2.0 / np.pi) * (v + 0.044715 * v**3)))


def striped8(idx):
    return np.concatenate([v.reshape(-1, 16).T for v in idx]).astype(np.uint16)


def unstriped8(offs):
    return np.stack([offs[16 * g:16 * g + 16].T.reshape(-1) for g in range(8)]).astype(np.int64)


def heads(h, wgt, idx8):
    r = np.arange(h.shape[0])
    return wgt[r // 4 % 128] * h[r[:, None], idx8[r % 512 // 64]]


def put_heads(h, wgs, idx8, t2):
    r = np.arange(h.shape[0])
    page = np.zeros((h.shape[0], t2))
    page[r[:, None], idx8[r % 512 // 64]] = wgs[r // 4 % 128] * h
    return page


K, H, N, T, S, T2, P = 1024, 512, 768, 4096, 1024, 2048, 1024

def setup_inputs():
    n = np.random.standard_normal
    s = mx_kscale(K)[:, None]
    u = mx_kscale(H)[:, None]
    d = {}
    d["tab_words"], d["tab_scales"] = pack_weight(n((K, T)) * s, "e4m3")
    d["offs"] = striped(np.random.permutation(T)[:S])
    d["wa"] = (1.5 * n((K, H)) / K**0.5 / s * u.T).astype(np.float32)
    d["wp_words"], d["wp_scales"] = pack_weight(0.34 * n((K, H)) / K**0.5 / s, "e2m1")
    d["phase0"] = np.random.uniform(-1.2, 1.2, H).astype(np.float32)
    d["lift"] = (0.6 * np.exp(0.3 * n(H)) * u[:, 0]).astype(np.float32)
    d["wgs"] = np.repeat(np.random.uniform(0.5, 2.0, (8, S)), 16, axis=0).astype(np.float32)
    d["offs2"] = striped8(np.stack([np.random.permutation(T2)[:S] for _ in range(8)]))
    d["wgt"] = np.repeat(np.random.uniform(0.5, 2.0, (8, P)), 16, axis=0).astype(np.float32)
    d["offs3"] = striped8(np.stack([np.random.permutation(T2)[:P] for _ in range(8)]))
    d["rain"] = (0.8 * n((H, P)) * u).astype(np.float32)
    d["w3"] = (n((H, N)) / H**0.5 / u).astype(np.float32)
    return d

def reference(tab_words, tab_scales, offs, wa, wp_words, wp_scales, phase0, lift, wgs, offs2, wgt, offs3, rain, w3):
    v = unpack_weight(tab_words, tab_scales, "e4m3")[:, unstriped(offs)]
    loud = mxq(f64(wa), 0, "e4m3").T @ v
    wp = unpack_weight(wp_words, wp_scales, "e2m1")
    phase = (wp.T @ v) + f64(phase0)[:, None]
    h = loud * np.sin(phase) + f64(lift)[:, None] * phase
    page = put_heads(h, f64(wgs), unstriped8(offs2), T2)
    x = heads(page, f64(wgt), unstriped8(offs3))
    z = x + f64(rain)
    return mxq(f64(w3), 0, "e4m3").T @ mxq(z, 0, "e4m3")

@@ -1,0 +1,304 @@
+import math
+from contextlib import ExitStack
+
+import concourse.mybir as mybir
+
+K, H, N, T, S, T2, M = 1024, 512, 768, 4096, 1024, 2048, 1024
+FLOPS = 2 * (2 * K * H * S + H * N * M)
+
+F32 = mybir.dt.float32
+BF16 = mybir.dt.bfloat16
+I32 = mybir.dt.int32
+U32 = mybir.dt.uint32
+U16 = mybir.dt.uint16
+U8 = mybir.dt.uint8
+FP8X4 = mybir.dt.float8_e4m3fn_x4
+FP4X4 = mybir.dt.float4_e2m1fn_x4
+ACT = mybir.ActivationFunctionType
+ALU = mybir.AluOpType
+
+P = 128
+HALF = 512
+UNITS = 8
+CHUNKS = [256, 256, 256, 128, 128]
+TWO_PI = 2.0 * math.pi
+
+
+def tile_list_frog_chorus_phase_kernel(
+    tc, tab_words, tab_scales, offs, wa, wp_words, wp_scales, phase0, lift, wgs, offs2, wgt, offs3, rain, w3, out
+):
+    nc = tc.nc
+    with ExitStack() as ctx:
+        keep = ctx.enter_context(tc.tile_pool(name="keep", bufs=1))
+        work = ctx.enter_context(tc.tile_pool(name="work", bufs=3))
+        psum = ctx.enter_context(tc.psum_pool(name="psum", bufs=1))
+
+        tab = [keep.tile([P, T], U32, name="tab%d" % a, align_bytes=64) for a in range(2)]
+        pick = keep.tile([P, S // 16], U16, name="pick")
+        put = keep.tile([P, S // 16], U16, name="put")
+        read = keep.tile([P, M // 16], U16, name="read")
+        wp_raw = keep.tile([P, 2, 2 * H], U8, name="wp_raw", align_bytes=64)
+        wa_raw = [keep.tile([P, 4, H], F32, name="wa_raw%d" % a, align_bytes=64) for a in range(2)]
+        wgs_sb = [keep.tile([P, HALF], F32, name="wgs%d" % h, align_bytes=64) for h in range(2)]
+        wgt_sb = keep.tile([P, M], F32, name="wgt", align_bytes=64)
+        w3_raw = keep.tile([P, 4, N], F32, name="w3_raw", align_bytes=64)
+        rain_sb = keep.tile([P, 4, M], F32, name="rain", align_bytes=64)
+
+        tab_sc = keep.tile([P, T], U8, name="tab_sc", align_bytes=64)
+        wp_sc_raw = keep.tile([P, 2, H], U8, name="wp_sc_raw", align_bytes=64)
+        picked_sc = keep.tile([P, S], U8, name="picked_sc", align_bytes=64)
+        v_sc = [keep.tile([P, S], U8, name="v_sc%d" % a, align_bytes=64) for a in range(2)]
+        ph0 = keep.tile([P, 4], F32, name="ph0")
+        lift_sb = keep.tile([P, 4], F32, name="lift")
+        nc.vector.memset(wp_sc_raw[:].bitcast(I32), 0)
+        nc.vector.memset(tab_sc[32:64, :].bitcast(I32), 0)
+        nc.vector.memset(tab_sc[64:128, :].bitcast(I32), 0)
+        for a in range(2):
+            nc.vector.memset(v_sc[a][:].bitcast(I32), 0)
+        nc.sync.dma_start(tab_sc[0:32, :].bitcast(I32), tab_scales.rearrange("a q t -> (a q) t").bitcast(I32))
+        nc.sync.dma_start(pick[:], offs)
+        nc.sync.dma_start(wp_raw[:].bitcast(I32), wp_words.rearrange("a p c -> p a c").bitcast(I32))
+        nc.sync.dma_start(tab[0][:].bitcast(I32), tab_words[0].rearrange("p t i -> p (t i)").bitcast(I32))
+        nc.sync.dma_start(ph0[:], phase0.rearrange("(p t) -> p t", t=4))
+        nc.sync.dma_start(lift_sb[:], lift.rearrange("(p t) -> p t", t=4))
+        nc.sync.dma_start(tab[1][:].bitcast(I32), tab_words[1].rearrange("p t i -> p (t i)").bitcast(I32))
+        for a in range(2):
+            nc.sync.dma_start(wa_raw[a][:], wa[a * 512 : (a + 1) * 512, :].rearrange("(p j) c -> p j c", j=4))
+        nc.sync.dma_start(put[:], offs2)
+        for h in range(2):
+            nc.sync.dma_start(wgs_sb[h][:], wgs[:, h * HALF : (h + 1) * HALF])
+        nc.sync.dma_start(read[:], offs3)
+        nc.sync.dma_start(wgt_sb[:], wgt)
+        nc.sync.dma_start(w3_raw[:], w3.rearrange("(p j) n -> p j n", j=4))
+        nc.sync.dma_start(rain_sb[:], rain.rearrange("(p j) m -> p j m", j=4))
+
+        for q in range(4):
+            nc.gpsimd.dma_start(
+                wp_sc_raw[32 * q : 32 * q + 4, :, :].bitcast(I32),
+                wp_scales[:, 4 * q : 4 * q + 4, :].rearrange("a r c -> r a c").bitcast(I32),
+            )
+
+        pages = [keep.tile([P, T2], F32, name="page%d" % i, align_bytes=64) for i in range(2)]
+        for page in pages:
+            nc.vector.memset(page[:], 0.0)
+
+        warm_in = keep.tile([P, 1], F32, name="warm_in")
+        warm_out = keep.tile([P, 1], F32, name="warm_out")
+        nc.gpsimd.memset(warm_in[:], 0.0)
+        nc.scalar.activation(warm_out[:], warm_in[:], ACT.Sin)
+
+        nc.vector.tensor_copy(picked_sc[:], tab_sc[:].indirect(pick[:]))
+        for a in range(2):
+            for q in range(4):
+                row = 16 * a + 4 * q
+                nc.gpsimd.dma_start(
+                    v_sc[a][32 * q : 32 * q + 4, :].bitcast(I32), picked_sc[row : row + 4, :].bitcast(I32)
+                )
+        wp = keep.tile([P, 2, 4, 2 * P], U8, name="wp", align_bytes=64)
+        wp_sc = keep.tile([P, 2, 4, P], U8, name="wp_sc", align_bytes=64)
+        nc.vector.tensor_copy(
+            wp[:].rearrange("p a t (m b) -> p a t m b", b=2), wp_raw[:].rearrange("p a (m t b) -> p a t m b", t=4, b=2)
+        )
+        v = [[keep.tile([P, HALF], U32, name="v%d_%d" % (a, h), align_bytes=64) for h in range(2)] for a in range(2)]
+
+        def gather_words(a, h):
+            nc.vector.tensor_copy(v[a][h][:], tab[a][:].indirect(pick[:, 32 * h : 32 * (h + 1)]))
+
+        gather_words(0, 0)
+        gather_words(0, 1)
+
+        nc.vector.tensor_copy(wp_sc[:], wp_sc_raw[:].rearrange("p a (m t) -> p a t m", t=4))
+        cos_bias = keep.tile([P, 4], F32, name="cos_bias")
+        lift_bias = keep.tile([P, 4], F32, name="lift_bias")
+        nc.vector.tensor_scalar_add(cos_bias[:], ph0[:], -0.5 * math.pi)
+        nc.vector.tensor_tensor(lift_bias[:], ph0[:], lift_sb[:], ALU.mult)
+
+        gather_words(1, 0)
+        gather_words(1, 1)
+
+        folded, turns, lifted, sines, hs = {}, {}, {}, {}, {}
+
+        def phase(u):
+            t, h = divmod(u, 2)
+            acc = psum.tile([P, HALF], F32, name="acc_p", tag="acc_p", bufs=3)
+            for a in range(2):
+                nc.tensor.matmul_mx(
+                    out=acc[:],
+                    lhsT=wp[:, a, t, :].bitcast(FP4X4),
+                    lhsT_scale=wp_sc[:, a, t, :],
+                    rhs=v[a][h][:].bitcast(FP8X4),
+                    rhs_scale=v_sc[a][:, h * HALF : (h + 1) * HALF],
+                    start=(a == 0),
+                    stop=(a == 1),
+                )
+            folded[u] = work.tile([P, HALF], F32, name="folded", tag="folded")
+            turns[u] = work.tile([P, HALF], U32, name="turns", tag="turns", bufs=2)
+            lifted[u] = work.tile([P, HALF], F32, name="lifted", tag="lifted", bufs=4)
+            nc.scalar.activation(folded[u][:], acc[:], ACT.Abs, bias=cos_bias[:, t : t + 1])
+            nc.scalar.activation(turns[u][:], folded[u][:], ACT.Copy, scale=1.0 / TWO_PI)
+            nc.scalar.activation(
+                lifted[u][:], acc[:], ACT.Identity, bias=lift_bias[:, t : t + 1], scale=lift_sb[:, t : t + 1]
+            )
+
+        def sine(u):
+            rest = work.tile([P, HALF], F32, name="rest", tag="rest")
+            size = work.tile([P, HALF], F32, name="size", tag="size", bufs=2)
+            sines[u] = work.tile([P, HALF], F32, name="sine", tag="sine")
+            nc.vector.scalar_tensor_tensor(rest[:], turns[u][:].bitcast(I32), -TWO_PI, folded[u][:], ALU.mult, ALU.add)
+            nc.scalar.activation(size[:], rest[:], ACT.Abs)
+            nc.scalar.activation(sines[u][:], size[:], ACT.Sin, bias=0.5 * math.pi, scale=-1.0)
+
+        wa_codes, wa_sc = {}, {}
+
+        def quantise_wa(a, t0, t1, engine):
+            n = t1 - t0
+            rounded = keep.tile([P, n, P, 4], BF16, name="wa_bf%d_%d" % (a, t0), align_bytes=64)
+            codes = keep.tile([P, n, P], U32, name="wa_codes%d_%d" % (a, t0), align_bytes=64)
+            scales = keep.tile([P, n, P], U8, name="wa_sc%d_%d" % (a, t0), align_bytes=64)
+            src = wa_raw[a][:].rearrange("p j (m t) -> p m j t", t=4)[:, :, :, t0:t1]
+            dst = rounded[:].rearrange("p t m j -> p m j t")
+            if engine == "vector":
+                nc.vector.tensor_copy(dst, src)
+            else:
+                nc.scalar.copy(dst, src)
+            nc.vector.quantize_mx(
+                out=codes[:].rearrange("p t m -> p (t m)").bitcast(FP8X4),
+                scales=scales[:].rearrange("p t m -> p (t m)"),
+                in_=rounded[:].rearrange("p t m j -> p (t m j)"),
+            )
+            for t in range(t0, t1):
+                wa_codes[a, t] = codes[:, t - t0, :]
+                wa_sc[a, t] = scales[:, t - t0, :]
+
+        gated = {}
+
+        def loud(u):
+            t, h = divmod(u, 2)
+            acc = psum.tile([P, HALF], F32, name="acc_l", tag="acc_l", bufs=2)
+            for a in range(2):
+                nc.tensor.matmul_mx(
+                    out=acc[:],
+                    lhsT=wa_codes[a, t].bitcast(FP8X4),
+                    lhsT_scale=wa_sc[a, t],
+                    rhs=v[a][h][:].bitcast(FP8X4),
+                    rhs_scale=v_sc[a][:, h * HALF : (h + 1) * HALF],
+                    start=(a == 0),
+                    stop=(a == 1),
+                )
+            gated[u] = work.tile([P, HALF], F32, name="gated", tag="gated")
+            nc.vector.tensor_tensor(gated[u][:], acc[:], sines[u][:], ALU.mult)
+
+        def combine(u):
+            hs[u] = work.tile([P, HALF], F32, name="h", tag="h")
+            nc.vector.tensor_tensor(hs[u][:], gated[u][:], lifted[u][:], ALU.add)
+
+        def scatter(u):
+            t, h = divmod(u, 2)
+            nc.vector.tensor_tensor(
+                pages[t % 2][:].indirect(put[:, 32 * h : 32 * (h + 1)]), hs[u][:], wgs_sb[h][:], ALU.mult
+            )
+
+        x = keep.tile([P, 4, M], F32, name="x", align_bytes=64)
+
+        def gather(t, m0, m1):
+            nc.vector.tensor_tensor(
+                x[:, t, m0:m1], pages[t % 2][:].indirect(read[:, m0 // 16 : m1 // 16]), wgt_sb[:, m0:m1], ALU.mult
+            )
+
+        w3_bf = keep.tile([P, N, 4], BF16, name="w3_bf", align_bytes=64)
+        w3_codes = keep.tile([P, N], U32, name="w3_codes", align_bytes=64)
+        w3_sc = keep.tile([P, N], U8, name="w3_sc", align_bytes=64)
+
+        def round_w3(n0, n1):
+            nc.scalar.copy(
+                w3_bf[:, n0:n1, :].rearrange("p (c i) j -> p c j i", i=4),
+                w3_raw[:, :, n0:n1].rearrange("p j (c i) -> p c j i", i=4),
+            )
+
+        def quantise_w3(n0, n1):
+            nc.vector.quantize_mx(
+                out=w3_codes[:, n0:n1].bitcast(FP8X4),
+                scales=w3_sc[:, n0:n1],
+                in_=w3_bf[:, n0:n1, :].rearrange("p n j -> p (n j)"),
+            )
+
+        phase(0)
+        phase(1)
+        quantise_wa(0, 0, 4, "vector")
+        sine(0)
+        phase(2)
+        quantise_wa(1, 0, 1, "vector")
+        sine(1)
+        loud(0)
+        quantise_wa(1, 1, 2, "scalar")
+        combine(0)
+        for u in range(UNITS):
+            if u + 1 < UNITS:
+                loud(u + 1)
+            if u + 2 < UNITS:
+                sine(u + 2)
+            if u + 3 < UNITS:
+                phase(u + 3)
+            if u == 0:
+                quantise_wa(1, 2, 4, "scalar")
+            if u + 1 < UNITS:
+                combine(u + 1)
+            scatter(u)
+            if u in (2, 3):
+                gather(0, (u - 2) * HALF, (u - 1) * HALF)
+            if u in (4, 5):
+                gather(1, (u - 4) * HALF, (u - 3) * HALF)
+            if u in (2, 3, 4):
+                round_w3((u - 2) * 256, (u - 1) * 256)
+            if u in (3, 4, 5):
+                quantise_w3((u - 3) * 256, (u - 2) * 256)
+
+        out_v = out.rearrange("(c p) m -> p c m", p=P)
+        zs = {}
+
+        def add_rain(c, m0, m1):
+            zs[c] = work.tile([P, m1 - m0, 4], BF16, name="z", tag="z", align_bytes=64)
+            nc.vector.tensor_tensor(
+                zs[c][:].rearrange("p (c i) t -> p c t i", i=4),
+                x[:, :, m0:m1].rearrange("p t (c i) -> p c t i", i=4),
+                rain_sb[:, :, m0:m1].rearrange("p t (c i) -> p c t i", i=4),
+                ALU.add,
+            )
+
+        def finish(c, m0, m1, last):
+            w = m1 - m0
+            codes = work.tile([P, w], U32, name="z_codes", tag="z_codes", align_bytes=64)
+            scales = work.tile([P, w], U8, name="z_sc", tag="z_sc", align_bytes=64)
+            nc.vector.quantize_mx(out=codes[:].bitcast(FP8X4), scales=scales[:], in_=zs[c][:].rearrange("p m t -> p (m t)"))
+            per = 2 if w == 256 else 3
+            for b in range(6 // per):
+                acc = psum.tile([P, per, w], F32, name="acc_o", tag="acc_o", bufs=3)
+                for i in range(per):
+                    n0 = (per * b + i) * P
+                    nc.tensor.matmul_mx(
+                        out=acc[:, i, :],
+                        lhsT=w3_codes[:, n0 : n0 + P].bitcast(FP8X4),
+                        lhsT_scale=w3_sc[:, n0 : n0 + P],
+                        rhs=codes[:].bitcast(FP8X4),
+                        rhs_scale=scales[:],
+                        start=True,
+                        stop=True,
+                    )
+                res = work.tile([P, per, w], F32, name="res", tag="res", bufs=4)
+                if last and b == 1:
+                    nc.vector.tensor_copy(res[:], acc[:])
+                else:
+                    nc.scalar.copy(res[:], acc[:])
+                nc.sync.dma_start(out_v[:, per * b : per * (b + 1), m0:m1], res[:])
+
+        edges = [sum(CHUNKS[:c]) for c in range(len(CHUNKS) + 1)]
+        last = len(CHUNKS) - 1
+        gather(2, edges[0], edges[1])
+        gather(3, edges[0], edges[1])
+        for c in range(len(CHUNKS)):
+            if c < last:
+                gather(2, edges[c + 1], edges[c + 2])
+            add_rain(c, edges[c], edges[c + 1])
+            if c < last:
+                gather(3, edges[c + 1], edges[c + 2])
+            finish(c, edges[c], edges[c + 1], c == last)

@@ -2,6 +2,7 @@ import math
 from contextlib import ExitStack
 
 import concourse.mybir as mybir
+from concourse.masks import make_identity
 
 K, H, N, T, S, T2, M = 1024, 512, 768, 4096, 1024, 2048, 1024
 FLOPS = 2 * (2 * K * H * S + H * N * M)
@@ -20,6 +21,7 @@ ALU = mybir.AluOpType
 P = 128
 HALF = 512
 UNITS = 8
+VECTOR_UNITS = 2
 CHUNKS = [256, 256, 256, 128, 128]
 TWO_PI = 2.0 * math.pi
 
@@ -33,54 +35,52 @@ def tile_list_frog_chorus_phase_kernel(
         work = ctx.enter_context(tc.tile_pool(name="work", bufs=3))
         psum = ctx.enter_context(tc.psum_pool(name="psum", bufs=1))
 
-        tab = [keep.tile([P, T], U32, name="tab%d" % a, align_bytes=64) for a in range(2)]
         pick = keep.tile([P, S // 16], U16, name="pick")
         put = keep.tile([P, S // 16], U16, name="put")
         read = keep.tile([P, M // 16], U16, name="read")
-        wp_raw = keep.tile([P, 2, 2 * H], U8, name="wp_raw", align_bytes=64)
-        wa_raw = [keep.tile([P, 4, H], F32, name="wa_raw%d" % a, align_bytes=64) for a in range(2)]
-        wgs_sb = [keep.tile([P, HALF], F32, name="wgs%d" % h, align_bytes=64) for h in range(2)]
-        wgt_sb = keep.tile([P, M], F32, name="wgt", align_bytes=64)
-        w3_raw = keep.tile([P, 4, N], F32, name="w3_raw", align_bytes=64)
-        rain_sb = keep.tile([P, 4, M], F32, name="rain", align_bytes=64)
-
-        tab_sc = keep.tile([P, T], U8, name="tab_sc", align_bytes=64)
-        wp_sc_raw = keep.tile([P, 2, H], U8, name="wp_sc_raw", align_bytes=64)
-        picked_sc = keep.tile([P, S], U8, name="picked_sc", align_bytes=64)
-        v_sc = [keep.tile([P, S], U8, name="v_sc%d" % a, align_bytes=64) for a in range(2)]
         ph0 = keep.tile([P, 4], F32, name="ph0")
         lift_sb = keep.tile([P, 4], F32, name="lift")
+        tab_sc = keep.tile([P, T], U8, name="tab_sc", align_bytes=64)
+        wp_raw = [
+            keep.tile([P, 2 * H], U8, name="wp_raw0", tag="slot_b", align_bytes=64),
+            keep.tile([P, 2 * H], U8, name="wp_raw1", tag="slot_c", align_bytes=64),
+        ]
+        picked_sc = keep.tile([P, S], U8, name="picked_sc", align_bytes=64)
+        tab0 = keep.tile([P, T], U32, name="tab0", align_bytes=64)
+        wp_sc_raw = keep.tile([P, 2, H], U8, name="wp_sc_raw", align_bytes=64)
+        v_sc = [keep.tile([P, S], U8, name="v_sc%d" % a, align_bytes=64) for a in range(2)]
+
+        def load_words(tile, a):
+            nc.sync.dma_start(tile[:].bitcast(I32), tab_words[a].rearrange("p t i -> p (t i)").bitcast(I32))
+
+        def load_wa(tile, a):
+            nc.sync.dma_start(tile[:], wa[a * 512 : (a + 1) * 512, :].rearrange("(p j) c -> p j c", j=4))
+
+        nc.sync.dma_start(tab_sc[0:32, :].bitcast(I32), tab_scales.rearrange("a q t -> (a q) t").bitcast(I32))
+        nc.sync.dma_start(pick[:], offs)
+        for a in range(2):
+            nc.sync.dma_start(wp_raw[a][:].bitcast(I32), wp_words[a].bitcast(I32))
+        nc.sync.dma_start(ph0[:], phase0.rearrange("(p t) -> p t", t=4))
+        nc.sync.dma_start(lift_sb[:], lift.rearrange("(p t) -> p t", t=4))
+        nc.sync.dma_start(put[:], offs2)
+        load_words(tab0, 0)
+        nc.sync.dma_start(read[:], offs3)
+        tab1 = keep.tile([P, T], U32, name="tab1", tag="slot_a", align_bytes=64)
+        load_words(tab1, 1)
+
         nc.vector.memset(wp_sc_raw[:].bitcast(I32), 0)
         nc.vector.memset(tab_sc[32:64, :].bitcast(I32), 0)
         nc.vector.memset(tab_sc[64:128, :].bitcast(I32), 0)
         for a in range(2):
             nc.vector.memset(v_sc[a][:].bitcast(I32), 0)
-        nc.sync.dma_start(tab_sc[0:32, :].bitcast(I32), tab_scales.rearrange("a q t -> (a q) t").bitcast(I32))
-        nc.sync.dma_start(pick[:], offs)
-        nc.sync.dma_start(wp_raw[:].bitcast(I32), wp_words.rearrange("a p c -> p a c").bitcast(I32))
-        nc.sync.dma_start(tab[0][:].bitcast(I32), tab_words[0].rearrange("p t i -> p (t i)").bitcast(I32))
-        nc.sync.dma_start(ph0[:], phase0.rearrange("(p t) -> p t", t=4))
-        nc.sync.dma_start(lift_sb[:], lift.rearrange("(p t) -> p t", t=4))
-        nc.sync.dma_start(tab[1][:].bitcast(I32), tab_words[1].rearrange("p t i -> p (t i)").bitcast(I32))
-        for a in range(2):
-            nc.sync.dma_start(wa_raw[a][:], wa[a * 512 : (a + 1) * 512, :].rearrange("(p j) c -> p j c", j=4))
-        nc.sync.dma_start(put[:], offs2)
-        for h in range(2):
-            nc.sync.dma_start(wgs_sb[h][:], wgs[:, h * HALF : (h + 1) * HALF])
-        nc.sync.dma_start(read[:], offs3)
-        nc.sync.dma_start(wgt_sb[:], wgt)
-        nc.sync.dma_start(w3_raw[:], w3.rearrange("(p j) n -> p j n", j=4))
-        nc.sync.dma_start(rain_sb[:], rain.rearrange("(p j) m -> p j m", j=4))
-
         for q in range(4):
             nc.gpsimd.dma_start(
                 wp_sc_raw[32 * q : 32 * q + 4, :, :].bitcast(I32),
                 wp_scales[:, 4 * q : 4 * q + 4, :].rearrange("a r c -> r a c").bitcast(I32),
             )
 
-        pages = [keep.tile([P, T2], F32, name="page%d" % i, align_bytes=64) for i in range(2)]
-        for page in pages:
-            nc.vector.memset(page[:], 0.0)
+        identity = keep.tile([P, P], F32, name="identity", align_bytes=64)
+        make_identity(nc, identity[:])
 
         warm_in = keep.tile([P, 1], F32, name="warm_in")
         warm_out = keep.tile([P, 1], F32, name="warm_out")
@@ -88,17 +88,35 @@ def tile_list_frog_chorus_phase_kernel(
         nc.scalar.activation(warm_out[:], warm_in[:], ACT.Sin)
 
         nc.vector.tensor_copy(picked_sc[:], tab_sc[:].indirect(pick[:]))
-        for a in range(2):
-            for q in range(4):
-                row = 16 * a + 4 * q
-                nc.gpsimd.dma_start(
-                    v_sc[a][32 * q : 32 * q + 4, :].bitcast(I32), picked_sc[row : row + 4, :].bitcast(I32)
-                )
+
+        def move_scales(a, q, queue):
+            row = 16 * a + 4 * q
+            queue.dma_start(v_sc[a][32 * q : 32 * q + 4, :].bitcast(I32), picked_sc[row : row + 4, :].bitcast(I32))
+
+        for a, q in [(0, 1), (0, 2), (0, 3), (1, 0), (1, 1), (1, 2)]:
+            move_scales(a, q, nc.sync)
+        move_scales(1, 3, nc.gpsimd)
+        nc.vector.tensor_copy(v_sc[0][0:4, :].bitcast(I32), picked_sc[0:4, :].bitcast(I32))
+        tab = [tab0, tab1]
+
         wp = keep.tile([P, 2, 4, 2 * P], U8, name="wp", align_bytes=64)
         wp_sc = keep.tile([P, 2, 4, P], U8, name="wp_sc", align_bytes=64)
-        nc.vector.tensor_copy(
-            wp[:].rearrange("p a t (m b) -> p a t m b", b=2), wp_raw[:].rearrange("p a (m t b) -> p a t m b", t=4, b=2)
-        )
+        for a in range(2):
+            nc.vector.tensor_copy(
+                wp[:, a].rearrange("p t (m b) -> p t m b", b=2),
+                wp_raw[a][:].rearrange("p (m t b) -> p t m b", t=4, b=2),
+            )
+        wa_raw = [
+            keep.tile([P, 4, H], F32, name="wa_raw0", tag="slot_b", align_bytes=64),
+            keep.tile([P, 4, H], F32, name="wa_raw1", tag="slot_c", align_bytes=64),
+        ]
+        load_wa(wa_raw[0], 0)
+        load_wa(wa_raw[1], 1)
+
+        pages = [keep.tile([P, T2], F32, name="page%d" % i, align_bytes=64) for i in range(2)]
+        for page in pages:
+            nc.vector.memset(page[:], 0.0)
+
         v = [[keep.tile([P, HALF], U32, name="v%d_%d" % (a, h), align_bytes=64) for h in range(2)] for a in range(2)]
 
         def gather_words(a, h):
@@ -115,12 +133,15 @@ def tile_list_frog_chorus_phase_kernel(
 
         gather_words(1, 0)
         gather_words(1, 1)
+        wgs_sb = keep.tile([P, S], F32, name="wgs", tag="slot_a", align_bytes=64)
+        for h in range(2):
+            nc.sync.dma_start(wgs_sb[:, h * HALF : (h + 1) * HALF], wgs[:, h * HALF : (h + 1) * HALF])
 
-        folded, turns, lifted, sines, hs = {}, {}, {}, {}, {}
+        lifted, sines, hs = {}, {}, {}
 
-        def phase(u):
+        def front(u):
             t, h = divmod(u, 2)
-            acc = psum.tile([P, HALF], F32, name="acc_p", tag="acc_p", bufs=3)
+            acc = psum.tile([P, HALF], F32, name="acc_p", tag="acc_p", bufs=2)
             for a in range(2):
                 nc.tensor.matmul_mx(
                     out=acc[:],
@@ -131,28 +152,48 @@ def tile_list_frog_chorus_phase_kernel(
                     start=(a == 0),
                     stop=(a == 1),
                 )
-            folded[u] = work.tile([P, HALF], F32, name="folded", tag="folded")
-            turns[u] = work.tile([P, HALF], U32, name="turns", tag="turns", bufs=2)
-            lifted[u] = work.tile([P, HALF], F32, name="lifted", tag="lifted", bufs=4)
-            nc.scalar.activation(folded[u][:], acc[:], ACT.Abs, bias=cos_bias[:, t : t + 1])
-            nc.scalar.activation(turns[u][:], folded[u][:], ACT.Copy, scale=1.0 / TWO_PI)
-            nc.scalar.activation(
-                lifted[u][:], acc[:], ACT.Identity, bias=lift_bias[:, t : t + 1], scale=lift_sb[:, t : t + 1]
-            )
-
-        def sine(u):
-            rest = work.tile([P, HALF], F32, name="rest", tag="rest")
+            folded = work.tile([P, HALF], F32, name="folded", tag="folded")
+            count = work.tile([P, HALF], U32, name="count", tag="count", bufs=2)
             size = work.tile([P, HALF], F32, name="size", tag="size", bufs=2)
-            sines[u] = work.tile([P, HALF], F32, name="sine", tag="sine")
-            nc.vector.scalar_tensor_tensor(rest[:], turns[u][:].bitcast(I32), -TWO_PI, folded[u][:], ALU.mult, ALU.add)
-            nc.scalar.activation(size[:], rest[:], ACT.Abs)
-            nc.scalar.activation(sines[u][:], size[:], ACT.Sin, bias=0.5 * math.pi, scale=-1.0)
+            lifted[u] = work.tile([P, HALF], F32, name="lifted", tag="lifted", bufs=4)
+            sines[u] = work.tile([P, HALF], F32, name="sine", tag="sine", bufs=4)
+
+            def lift_phase():
+                nc.scalar.activation(
+                    lifted[u][:], acc[:], ACT.Identity, bias=lift_bias[:, t : t + 1], scale=lift_sb[:, t : t + 1]
+                )
+
+            nc.scalar.activation(folded[:], acc[:], ACT.Abs, bias=cos_bias[:, t : t + 1])
+            nc.scalar.activation(count[:], folded[:], ACT.Copy, scale=1.0 / TWO_PI)
+            if u < VECTOR_UNITS:
+                rest = work.tile([P, HALF], F32, name="rest", tag="turns")
+                nc.vector.scalar_tensor_tensor(rest[:], count[:].bitcast(I32), -TWO_PI, folded[:], ALU.mult, ALU.add)
+                nc.scalar.activation(size[:], rest[:], ACT.Abs)
+                nc.scalar.activation(sines[u][:], size[:], ACT.Sin, bias=0.5 * math.pi, scale=-1.0)
+                lift_phase()
+            else:
+                turns = work.tile([P, HALF], F32, name="turns", tag="turns")
+                nc.scalar.activation(turns[:], count[:], ACT.Copy, scale=-TWO_PI)
+                lift_phase()
+                rest = psum.tile([P, HALF], F32, name="rest_t", tag="rest_t", bufs=2)
+                for b in range(4):
+                    cols = slice(b * P, (b + 1) * P)
+                    nc.tensor.matmul(rest[:, cols], folded[:, cols], identity[:], start=True, stop=False, is_transpose=True)
+                    nc.tensor.matmul(rest[:, cols], turns[:, cols], identity[:], start=False, stop=True, is_transpose=True)
+                turned = work.tile([P, HALF], F32, name="turned", tag="turned", bufs=2)
+                nc.scalar.activation(size[:], rest[:], ACT.Abs)
+                nc.scalar.activation(turned[:], size[:], ACT.Sin, bias=0.5 * math.pi, scale=-1.0)
+                back = psum.tile([P, HALF], F32, name="back", tag="bank%d" % (u % 4))
+                for b in range(4):
+                    cols = slice(b * P, (b + 1) * P)
+                    nc.tensor.transpose(back[:, cols], turned[:, cols], identity[:])
+                nc.scalar.copy(sines[u][:], back[:])
 
         wa_codes, wa_sc = {}, {}
 
         def quantise_wa(a, t0, t1, engine):
             n = t1 - t0
-            rounded = keep.tile([P, n, P, 4], BF16, name="wa_bf%d_%d" % (a, t0), align_bytes=64)
+            rounded = keep.tile([P, n, P, 4], BF16, name="wa_bf%d_%d" % (a, t0), tag="wa_bf%d_%d" % (a, t0), align_bytes=64)
             codes = keep.tile([P, n, P], U32, name="wa_codes%d_%d" % (a, t0), align_bytes=64)
             scales = keep.tile([P, n, P], U8, name="wa_sc%d_%d" % (a, t0), align_bytes=64)
             src = wa_raw[a][:].rearrange("p j (m t) -> p m j t", t=4)[:, :, :, t0:t1]
@@ -174,7 +215,7 @@ def tile_list_frog_chorus_phase_kernel(
 
         def loud(u):
             t, h = divmod(u, 2)
-            acc = psum.tile([P, HALF], F32, name="acc_l", tag="acc_l", bufs=2)
+            acc = psum.tile([P, HALF], F32, name="acc_l", tag="bank%d" % (u % 4))
             for a in range(2):
                 nc.tensor.matmul_mx(
                     out=acc[:],
@@ -195,7 +236,7 @@ def tile_list_frog_chorus_phase_kernel(
         def scatter(u):
             t, h = divmod(u, 2)
             nc.vector.tensor_tensor(
-                pages[t % 2][:].indirect(put[:, 32 * h : 32 * (h + 1)]), hs[u][:], wgs_sb[h][:], ALU.mult
+                pages[t % 2][:].indirect(put[:, 32 * h : 32 * (h + 1)]), hs[u][:], wgs_sb[:, h * HALF : (h + 1) * HALF], ALU.mult
             )
 
         x = keep.tile([P, 4, M], F32, name="x", align_bytes=64)
@@ -222,36 +263,35 @@ def tile_list_frog_chorus_phase_kernel(
                 in_=w3_bf[:, n0:n1, :].rearrange("p n j -> p (n j)"),
             )
 
-        phase(0)
-        phase(1)
+        front(0)
         quantise_wa(0, 0, 4, "vector")
-        sine(0)
-        phase(2)
+        wgt_sb = keep.tile([P, M], F32, name="wgt", tag="wa_bf0_0", align_bytes=64)
+        rain_sb = keep.tile([P, 4, M], F32, name="rain", tag="slot_b", align_bytes=64)
+        nc.sync.dma_start(wgt_sb[:], wgt)
+        nc.sync.dma_start(rain_sb[:], rain.rearrange("(p j) m -> p j m", j=4))
         quantise_wa(1, 0, 1, "vector")
-        sine(1)
+        front(1)
         loud(0)
-        quantise_wa(1, 1, 2, "scalar")
         combine(0)
+        quantise_wa(1, 1, 2, "vector")
+        quantise_wa(1, 2, 4, "vector")
+        w3_raw = keep.tile([P, 4, N], F32, name="w3_raw", tag="slot_c", align_bytes=64)
+        nc.sync.dma_start(w3_raw[:], w3.rearrange("(p j) n -> p j n", j=4))
         for u in range(UNITS):
+            if u + 2 < UNITS:
+                front(u + 2)
             if u + 1 < UNITS:
                 loud(u + 1)
-            if u + 2 < UNITS:
-                sine(u + 2)
-            if u + 3 < UNITS:
-                phase(u + 3)
-            if u == 0:
-                quantise_wa(1, 2, 4, "scalar")
+            scatter(u)
             if u + 1 < UNITS:
                 combine(u + 1)
-            scatter(u)
             if u in (2, 3):
                 gather(0, (u - 2) * HALF, (u - 1) * HALF)
             if u in (4, 5):
                 gather(1, (u - 4) * HALF, (u - 3) * HALF)
-            if u in (2, 3, 4):
-                round_w3((u - 2) * 256, (u - 1) * 256)
-            if u in (3, 4, 5):
-                quantise_w3((u - 3) * 256, (u - 2) * 256)
+        for n0 in range(0, N, 256):
+            round_w3(n0, n0 + 256)
+            quantise_w3(n0, n0 + 256)
 
         out_v = out.rearrange("(c p) m -> p c m", p=P)
         zs = {}
@@ -272,7 +312,7 @@ def tile_list_frog_chorus_phase_kernel(
             nc.vector.quantize_mx(out=codes[:].bitcast(FP8X4), scales=scales[:], in_=zs[c][:].rearrange("p m t -> p (m t)"))
             per = 2 if w == 256 else 3
             for b in range(6 // per):
-                acc = psum.tile([P, per, w], F32, name="acc_o", tag="acc_o", bufs=3)
+                acc = psum.tile([P, per, w], F32, name="acc_o", tag="bank%d" % ((3 * c + b) % 4))
                 for i in range(per):
                     n0 = (per * b + i) * P
                     nc.tensor.matmul_mx(
@@ -284,7 +324,7 @@ def tile_list_frog_chorus_phase_kernel(
                         start=True,
                         stop=True,
                     )
-                res = work.tile([P, per, w], F32, name="res", tag="res", bufs=4)
+                res = work.tile([P, per, w], F32, name="res", tag="res", bufs=8)
                 if last and b == 1:
                     nc.vector.tensor_copy(res[:], acc[:])
                 else:

@@ -19,11 +19,14 @@ ACT = mybir.ActivationFunctionType
 ALU = mybir.AluOpType
 
 P = 128
+K_PASS = 512
 HALF = 512
-UNITS = 8
-VECTOR_UNITS = 2
-CHUNKS = [256, 256, 256, 128, 128]
+PER_COLUMN = 16
 TWO_PI = 2.0 * math.pi
+VECTOR_UNITS = 2
+SHARED_BANKS = 4
+W3_STEP = 256
+CHUNKS = [256, 256, 256, 128, 128]
 
 
 def tile_list_frog_chorus_phase_kernel(
@@ -35,18 +38,18 @@ def tile_list_frog_chorus_phase_kernel(
         work = ctx.enter_context(tc.tile_pool(name="work", bufs=3))
         psum = ctx.enter_context(tc.psum_pool(name="psum", bufs=1))
 
-        pick = keep.tile([P, S // 16], U16, name="pick")
-        put = keep.tile([P, S // 16], U16, name="put")
-        read = keep.tile([P, M // 16], U16, name="read")
-        ph0 = keep.tile([P, 4], F32, name="ph0")
-        lift_sb = keep.tile([P, 4], F32, name="lift")
+        pick = keep.tile([P, S // PER_COLUMN], U16, name="pick")
+        put = keep.tile([P, S // PER_COLUMN], U16, name="put")
+        read = keep.tile([P, M // PER_COLUMN], U16, name="read")
+        phase0_sb = keep.tile([P, 4], F32, name="phase0_sb")
+        lift_sb = keep.tile([P, 4], F32, name="lift_sb")
         tab_sc = keep.tile([P, T], U8, name="tab_sc", align_bytes=64)
         wp_raw = [
             keep.tile([P, 2 * H], U8, name="wp_raw0", tag="slot_b", align_bytes=64),
             keep.tile([P, 2 * H], U8, name="wp_raw1", tag="slot_c", align_bytes=64),
         ]
         picked_sc = keep.tile([P, S], U8, name="picked_sc", align_bytes=64)
-        tab0 = keep.tile([P, T], U32, name="tab0", align_bytes=64)
+        tab0 = keep.tile([P, T], U32, name="tab0", tag="slot_e", align_bytes=64)
         wp_sc_raw = keep.tile([P, 2, H], U8, name="wp_sc_raw", align_bytes=64)
         v_sc = [keep.tile([P, S], U8, name="v_sc%d" % a, align_bytes=64) for a in range(2)]
 
@@ -54,13 +57,13 @@ def tile_list_frog_chorus_phase_kernel(
             nc.sync.dma_start(tile[:].bitcast(I32), tab_words[a].rearrange("p t i -> p (t i)").bitcast(I32))
 
         def load_wa(tile, a):
-            nc.sync.dma_start(tile[:], wa[a * 512 : (a + 1) * 512, :].rearrange("(p j) c -> p j c", j=4))
+            nc.sync.dma_start(tile[:], wa[a * K_PASS : (a + 1) * K_PASS, :].rearrange("(p j) c -> p j c", j=4))
 
         nc.sync.dma_start(tab_sc[0:32, :].bitcast(I32), tab_scales.rearrange("a q t -> (a q) t").bitcast(I32))
         nc.sync.dma_start(pick[:], offs)
         for a in range(2):
             nc.sync.dma_start(wp_raw[a][:].bitcast(I32), wp_words[a].bitcast(I32))
-        nc.sync.dma_start(ph0[:], phase0.rearrange("(p t) -> p t", t=4))
+        nc.sync.dma_start(phase0_sb[:], phase0.rearrange("(p t) -> p t", t=4))
         nc.sync.dma_start(lift_sb[:], lift.rearrange("(p t) -> p t", t=4))
         nc.sync.dma_start(put[:], offs2)
         load_words(tab0, 0)
@@ -82,20 +85,12 @@ def tile_list_frog_chorus_phase_kernel(
         identity = keep.tile([P, P], F32, name="identity", align_bytes=64)
         make_identity(nc, identity[:])
 
-        warm_in = keep.tile([P, 1], F32, name="warm_in")
-        warm_out = keep.tile([P, 1], F32, name="warm_out")
-        nc.gpsimd.memset(warm_in[:], 0.0)
-        nc.scalar.activation(warm_out[:], warm_in[:], ACT.Sin)
-
         nc.vector.tensor_copy(picked_sc[:], tab_sc[:].indirect(pick[:]))
-
-        def move_scales(a, q, queue):
+        moves = [(a, q) for a in range(2) for q in range(4)][1:]
+        for a, q in moves:
+            queue = nc.gpsimd if (a, q) == moves[-1] else nc.sync
             row = 16 * a + 4 * q
             queue.dma_start(v_sc[a][32 * q : 32 * q + 4, :].bitcast(I32), picked_sc[row : row + 4, :].bitcast(I32))
-
-        for a, q in [(0, 1), (0, 2), (0, 3), (1, 0), (1, 1), (1, 2)]:
-            move_scales(a, q, nc.sync)
-        move_scales(1, 3, nc.gpsimd)
         nc.vector.tensor_copy(v_sc[0][0:4, :].bitcast(I32), picked_sc[0:4, :].bitcast(I32))
         tab = [tab0, tab1]
 
@@ -103,8 +98,8 @@ def tile_list_frog_chorus_phase_kernel(
         wp_sc = keep.tile([P, 2, 4, P], U8, name="wp_sc", align_bytes=64)
         for a in range(2):
             nc.vector.tensor_copy(
-                wp[:, a].rearrange("p t (m b) -> p t m b", b=2),
-                wp_raw[a][:].rearrange("p (m t b) -> p t m b", t=4, b=2),
+                wp[:, a].bitcast(U16),
+                wp_raw[a][:].bitcast(U16).rearrange("p (m t) -> p t m", t=4),
             )
         wa_raw = [
             keep.tile([P, 4, H], F32, name="wa_raw0", tag="slot_b", align_bytes=64),
@@ -113,33 +108,42 @@ def tile_list_frog_chorus_phase_kernel(
         load_wa(wa_raw[0], 0)
         load_wa(wa_raw[1], 1)
 
-        pages = [keep.tile([P, T2], F32, name="page%d" % i, align_bytes=64) for i in range(2)]
-        for page in pages:
-            nc.vector.memset(page[:], 0.0)
+        page0 = keep.tile([P, T2], F32, name="page0", align_bytes=64)
+        nc.vector.memset(page0[:], 0.0)
 
         v = [[keep.tile([P, HALF], U32, name="v%d_%d" % (a, h), align_bytes=64) for h in range(2)] for a in range(2)]
 
+        def entries(j0, j1):
+            return slice(j0 // PER_COLUMN, j1 // PER_COLUMN)
+
         def gather_words(a, h):
-            nc.vector.tensor_copy(v[a][h][:], tab[a][:].indirect(pick[:, 32 * h : 32 * (h + 1)]))
+            nc.vector.tensor_copy(v[a][h][:], tab[a][:].indirect(pick[:, entries(h * HALF, (h + 1) * HALF)]))
 
         gather_words(0, 0)
         gather_words(0, 1)
+        page1 = keep.tile([P, T2], F32, name="page1", tag="slot_e", align_bytes=64)
+        nc.vector.memset(page1[:], 0.0)
+        pages = [page0, page1]
 
         nc.vector.tensor_copy(wp_sc[:], wp_sc_raw[:].rearrange("p a (m t) -> p a t m", t=4))
         cos_bias = keep.tile([P, 4], F32, name="cos_bias")
         lift_bias = keep.tile([P, 4], F32, name="lift_bias")
-        nc.vector.tensor_scalar_add(cos_bias[:], ph0[:], -0.5 * math.pi)
-        nc.vector.tensor_tensor(lift_bias[:], ph0[:], lift_sb[:], ALU.mult)
+        nc.vector.tensor_scalar_add(cos_bias[:], phase0_sb[:], -0.5 * math.pi)
+        nc.vector.tensor_tensor(lift_bias[:], phase0_sb[:], lift_sb[:], ALU.mult)
 
         gather_words(1, 0)
         gather_words(1, 1)
-        wgs_sb = keep.tile([P, S], F32, name="wgs", tag="slot_a", align_bytes=64)
+        wgs_sb = keep.tile([P, S], F32, name="wgs_sb", tag="slot_a", align_bytes=64)
         for h in range(2):
             nc.sync.dma_start(wgs_sb[:, h * HALF : (h + 1) * HALF], wgs[:, h * HALF : (h + 1) * HALF])
 
-        lifted, sines, hs = {}, {}, {}
+        lifted, sines, gated, hs = {}, {}, {}, {}
+        wa_codes, wa_sc = {}, {}
 
-        def front(u):
+        def shared_bank(i):
+            return "bank%d" % (i % SHARED_BANKS)
+
+        def phase_terms(u):
             t, h = divmod(u, 2)
             acc = psum.tile([P, HALF], F32, name="acc_p", tag="acc_p", bufs=2)
             for a in range(2):
@@ -155,12 +159,17 @@ def tile_list_frog_chorus_phase_kernel(
             folded = work.tile([P, HALF], F32, name="folded", tag="folded")
             count = work.tile([P, HALF], U32, name="count", tag="count", bufs=2)
             size = work.tile([P, HALF], F32, name="size", tag="size", bufs=2)
-            lifted[u] = work.tile([P, HALF], F32, name="lifted", tag="lifted", bufs=4)
+            if h == 0:
+                lifted[t] = work.tile([P, S], F32, name="lifted", tag="lifted")
             sines[u] = work.tile([P, HALF], F32, name="sine", tag="sine", bufs=4)
 
             def lift_phase():
                 nc.scalar.activation(
-                    lifted[u][:], acc[:], ACT.Identity, bias=lift_bias[:, t : t + 1], scale=lift_sb[:, t : t + 1]
+                    lifted[t][:, h * HALF : (h + 1) * HALF],
+                    acc[:],
+                    ACT.Identity,
+                    bias=lift_bias[:, t : t + 1],
+                    scale=lift_sb[:, t : t + 1],
                 )
 
             nc.scalar.activation(folded[:], acc[:], ACT.Abs, bias=cos_bias[:, t : t + 1])
@@ -175,33 +184,31 @@ def tile_list_frog_chorus_phase_kernel(
                 turns = work.tile([P, HALF], F32, name="turns", tag="turns")
                 nc.scalar.activation(turns[:], count[:], ACT.Copy, scale=-TWO_PI)
                 lift_phase()
-                rest = psum.tile([P, HALF], F32, name="rest_t", tag="rest_t", bufs=2)
-                for b in range(4):
-                    cols = slice(b * P, (b + 1) * P)
-                    nc.tensor.matmul(rest[:, cols], folded[:, cols], identity[:], start=True, stop=False, is_transpose=True)
-                    nc.tensor.matmul(rest[:, cols], turns[:, cols], identity[:], start=False, stop=True, is_transpose=True)
-                turned = work.tile([P, HALF], F32, name="turned", tag="turned", bufs=2)
-                nc.scalar.activation(size[:], rest[:], ACT.Abs)
-                nc.scalar.activation(turned[:], size[:], ACT.Sin, bias=0.5 * math.pi, scale=-1.0)
-                back = psum.tile([P, HALF], F32, name="back", tag="bank%d" % (u % 4))
-                for b in range(4):
-                    cols = slice(b * P, (b + 1) * P)
-                    nc.tensor.transpose(back[:, cols], turned[:, cols], identity[:])
+                rest_t = psum.tile([P, HALF], F32, name="rest_t", tag="rest_t", bufs=2)
+                for j0 in range(0, HALF, P):
+                    cols = slice(j0, j0 + P)
+                    for term, first in ((folded, True), (turns, False)):
+                        nc.tensor.matmul(
+                            rest_t[:, cols], term[:, cols], identity[:], start=first, stop=not first, is_transpose=True
+                        )
+                sine_t = work.tile([P, HALF], F32, name="sine_t", tag="sine_t", bufs=2)
+                nc.scalar.activation(size[:], rest_t[:], ACT.Abs)
+                nc.scalar.activation(sine_t[:], size[:], ACT.Sin, bias=0.5 * math.pi, scale=-1.0)
+                back = psum.tile([P, HALF], F32, name="back", tag=shared_bank(u))
+                for j0 in range(0, HALF, P):
+                    nc.tensor.transpose(back[:, j0 : j0 + P], sine_t[:, j0 : j0 + P], identity[:])
                 nc.scalar.copy(sines[u][:], back[:])
 
-        wa_codes, wa_sc = {}, {}
-
-        def quantise_wa(a, t0, t1, engine):
+        def quantise_wa(a, t0, t1):
             n = t1 - t0
-            rounded = keep.tile([P, n, P, 4], BF16, name="wa_bf%d_%d" % (a, t0), tag="wa_bf%d_%d" % (a, t0), align_bytes=64)
-            codes = keep.tile([P, n, P], U32, name="wa_codes%d_%d" % (a, t0), align_bytes=64)
-            scales = keep.tile([P, n, P], U8, name="wa_sc%d_%d" % (a, t0), align_bytes=64)
-            src = wa_raw[a][:].rearrange("p j (m t) -> p m j t", t=4)[:, :, :, t0:t1]
-            dst = rounded[:].rearrange("p t m j -> p m j t")
-            if engine == "vector":
-                nc.vector.tensor_copy(dst, src)
-            else:
-                nc.scalar.copy(dst, src)
+            label = "%d_%d" % (a, t0)
+            rounded = keep.tile([P, n, P, 4], BF16, name="wa_bf" + label, tag="wa_bf" + label, align_bytes=64)
+            codes = keep.tile([P, n, P], U32, name="wa_codes" + label, align_bytes=64)
+            scales = keep.tile([P, n, P], U8, name="wa_sc" + label, align_bytes=64)
+            nc.vector.tensor_copy(
+                rounded[:].rearrange("p t m j -> p m j t"),
+                wa_raw[a][:].rearrange("p j (m t) -> p m j t", t=4)[:, :, :, t0:t1],
+            )
             nc.vector.quantize_mx(
                 out=codes[:].rearrange("p t m -> p (t m)").bitcast(FP8X4),
                 scales=scales[:].rearrange("p t m -> p (t m)"),
@@ -211,11 +218,9 @@ def tile_list_frog_chorus_phase_kernel(
                 wa_codes[a, t] = codes[:, t - t0, :]
                 wa_sc[a, t] = scales[:, t - t0, :]
 
-        gated = {}
-
         def loud(u):
             t, h = divmod(u, 2)
-            acc = psum.tile([P, HALF], F32, name="acc_l", tag="bank%d" % (u % 4))
+            acc = psum.tile([P, HALF], F32, name="acc_l", tag=shared_bank(u))
             for a in range(2):
                 nc.tensor.matmul_mx(
                     out=acc[:],
@@ -226,95 +231,109 @@ def tile_list_frog_chorus_phase_kernel(
                     start=(a == 0),
                     stop=(a == 1),
                 )
-            gated[u] = work.tile([P, HALF], F32, name="gated", tag="gated")
-            nc.vector.tensor_tensor(gated[u][:], acc[:], sines[u][:], ALU.mult)
+            if h == 0:
+                gated[t] = work.tile([P, S], F32, name="gated", tag="gated", bufs=2)
+            nc.vector.tensor_tensor(gated[t][:, h * HALF : (h + 1) * HALF], acc[:], sines[u][:], ALU.mult)
 
-        def combine(u):
-            hs[u] = work.tile([P, HALF], F32, name="h", tag="h")
-            nc.vector.tensor_tensor(hs[u][:], gated[u][:], lifted[u][:], ALU.add)
+        def combine(t, j0, j1):
+            if j0 == 0:
+                hs[t] = work.tile([P, S], F32, name="h", tag="h", bufs=2)
+            nc.vector.tensor_tensor(hs[t][:, j0:j1], gated[t][:, j0:j1], lifted[t][:, j0:j1], ALU.add)
 
-        def scatter(u):
-            t, h = divmod(u, 2)
+        def scatter(t, j0, j1):
             nc.vector.tensor_tensor(
-                pages[t % 2][:].indirect(put[:, 32 * h : 32 * (h + 1)]), hs[u][:], wgs_sb[:, h * HALF : (h + 1) * HALF], ALU.mult
+                pages[t % 2][:].indirect(put[:, entries(j0, j1)]), hs[t][:, j0:j1], wgs_sb[:, j0:j1], ALU.mult
             )
+
+        def unit_columns(u):
+            t, h = divmod(u, 2)
+            return t, h * HALF, (h + 1) * HALF
 
         x = keep.tile([P, 4, M], F32, name="x", align_bytes=64)
 
         def gather(t, m0, m1):
             nc.vector.tensor_tensor(
-                x[:, t, m0:m1], pages[t % 2][:].indirect(read[:, m0 // 16 : m1 // 16]), wgt_sb[:, m0:m1], ALU.mult
+                x[:, t, m0:m1], pages[t % 2][:].indirect(read[:, entries(m0, m1)]), wgt_sb[:, m0:m1], ALU.mult
             )
 
         w3_bf = keep.tile([P, N, 4], BF16, name="w3_bf", align_bytes=64)
         w3_codes = keep.tile([P, N], U32, name="w3_codes", align_bytes=64)
         w3_sc = keep.tile([P, N], U8, name="w3_sc", align_bytes=64)
 
-        def round_w3(n0, n1):
+        def quantise_w3(n0, n1):
             nc.scalar.copy(
                 w3_bf[:, n0:n1, :].rearrange("p (c i) j -> p c j i", i=4),
                 w3_raw[:, :, n0:n1].rearrange("p j (c i) -> p c j i", i=4),
             )
-
-        def quantise_w3(n0, n1):
             nc.vector.quantize_mx(
                 out=w3_codes[:, n0:n1].bitcast(FP8X4),
                 scales=w3_sc[:, n0:n1],
                 in_=w3_bf[:, n0:n1, :].rearrange("p n j -> p (n j)"),
             )
 
-        front(0)
-        quantise_wa(0, 0, 4, "vector")
-        wgt_sb = keep.tile([P, M], F32, name="wgt", tag="wa_bf0_0", align_bytes=64)
-        rain_sb = keep.tile([P, 4, M], F32, name="rain", tag="slot_b", align_bytes=64)
+        phase_terms(0)
+        quantise_wa(0, 0, 4)
+        wgt_sb = keep.tile([P, M], F32, name="wgt_sb", tag="wa_bf0_0", align_bytes=64)
+        rain_sb = keep.tile([P, 4, M], F32, name="rain_sb", tag="slot_b", align_bytes=64)
         nc.sync.dma_start(wgt_sb[:], wgt)
         nc.sync.dma_start(rain_sb[:], rain.rearrange("(p j) m -> p j m", j=4))
-        quantise_wa(1, 0, 1, "vector")
-        front(1)
+        quantise_wa(1, 0, 1)
+        phase_terms(1)
         loud(0)
-        combine(0)
-        quantise_wa(1, 1, 2, "vector")
-        quantise_wa(1, 2, 4, "vector")
+        combine(*unit_columns(0))
+        quantise_wa(1, 1, 2)
+        quantise_wa(1, 2, 4)
         w3_raw = keep.tile([P, 4, N], F32, name="w3_raw", tag="slot_c", align_bytes=64)
         nc.sync.dma_start(w3_raw[:], w3.rearrange("(p j) n -> p j n", j=4))
-        for u in range(UNITS):
-            if u + 2 < UNITS:
-                front(u + 2)
-            if u + 1 < UNITS:
-                loud(u + 1)
-            scatter(u)
-            if u + 1 < UNITS:
-                combine(u + 1)
-            if u in (2, 3):
-                gather(0, (u - 2) * HALF, (u - 1) * HALF)
-            if u in (4, 5):
-                gather(1, (u - 4) * HALF, (u - 3) * HALF)
-        for n0 in range(0, N, 256):
-            round_w3(n0, n0 + 256)
-            quantise_w3(n0, n0 + 256)
+
+        for u in range(4):
+            phase_terms(u + 2)
+            loud(u + 1)
+            scatter(*unit_columns(u))
+            if u + 1 < 4:
+                combine(*unit_columns(u + 1))
+            if u + 1 == 3:
+                gather(0, 0, M)
+
+        phase_terms(6)
+        loud(5)
+        phase_terms(7)
+        gather(1, 0, M)
+        combine(2, 0, S)
+        loud(6)
+        scatter(2, 0, S)
+        loud(7)
+        for n0 in range(0, N, W3_STEP):
+            quantise_w3(n0, n0 + W3_STEP)
+        combine(3, 0, S)
+        gather(2, 0, CHUNKS[0])
+        scatter(3, 0, S)
 
         out_v = out.rearrange("(c p) m -> p c m", p=P)
-        zs = {}
+        edges = [sum(CHUNKS[:c]) for c in range(len(CHUNKS) + 1)]
+        last = len(CHUNKS) - 1
 
-        def add_rain(c, m0, m1):
-            zs[c] = work.tile([P, m1 - m0, 4], BF16, name="z", tag="z", align_bytes=64)
+        def add_rain(m0, m1):
+            z = work.tile([P, m1 - m0, 4], BF16, name="z", tag="z", align_bytes=64)
             nc.vector.tensor_tensor(
-                zs[c][:].rearrange("p (c i) t -> p c t i", i=4),
+                z[:].rearrange("p (c i) t -> p c t i", i=4),
                 x[:, :, m0:m1].rearrange("p t (c i) -> p c t i", i=4),
                 rain_sb[:, :, m0:m1].rearrange("p t (c i) -> p c t i", i=4),
                 ALU.add,
             )
+            return z
 
-        def finish(c, m0, m1, last):
+        def finish(c, z):
+            m0, m1 = edges[c], edges[c + 1]
             w = m1 - m0
             codes = work.tile([P, w], U32, name="z_codes", tag="z_codes", align_bytes=64)
             scales = work.tile([P, w], U8, name="z_sc", tag="z_sc", align_bytes=64)
-            nc.vector.quantize_mx(out=codes[:].bitcast(FP8X4), scales=scales[:], in_=zs[c][:].rearrange("p m t -> p (m t)"))
-            per = 2 if w == 256 else 3
-            for b in range(6 // per):
-                acc = psum.tile([P, per, w], F32, name="acc_o", tag="bank%d" % ((3 * c + b) % 4))
-                for i in range(per):
-                    n0 = (per * b + i) * P
+            nc.vector.quantize_mx(out=codes[:].bitcast(FP8X4), scales=scales[:], in_=z[:].rearrange("p m t -> p (m t)"))
+            per_bank = 2 if w == CHUNKS[0] else 3
+            for b in range(N // P // per_bank):
+                acc = psum.tile([P, per_bank, w], F32, name="acc_o", tag=shared_bank(3 * c + b))
+                for i in range(per_bank):
+                    n0 = (per_bank * b + i) * P
                     nc.tensor.matmul_mx(
                         out=acc[:, i, :],
                         lhsT=w3_codes[:, n0 : n0 + P].bitcast(FP8X4),
@@ -324,21 +343,18 @@ def tile_list_frog_chorus_phase_kernel(
                         start=True,
                         stop=True,
                     )
-                res = work.tile([P, per, w], F32, name="res", tag="res", bufs=8)
-                if last and b == 1:
+                res = work.tile([P, per_bank, w], F32, name="res", tag="res", bufs=8)
+                if c == last and b == 1:
                     nc.vector.tensor_copy(res[:], acc[:])
                 else:
                     nc.scalar.copy(res[:], acc[:])
-                nc.sync.dma_start(out_v[:, per * b : per * (b + 1), m0:m1], res[:])
+                nc.sync.dma_start(out_v[:, per_bank * b : per_bank * (b + 1), m0:m1], res[:])
 
-        edges = [sum(CHUNKS[:c]) for c in range(len(CHUNKS) + 1)]
-        last = len(CHUNKS) - 1
-        gather(2, edges[0], edges[1])
         gather(3, edges[0], edges[1])
         for c in range(len(CHUNKS)):
             if c < last:
                 gather(2, edges[c + 1], edges[c + 2])
-            add_rain(c, edges[c], edges[c + 1])
+            z = add_rain(edges[c], edges[c + 1])
             if c < last:
                 gather(3, edges[c + 1], edges[c + 2])
-            finish(c, edges[c], edges[c + 1], c == last)
+            finish(c, z)

import math
from contextlib import ExitStack

import concourse.mybir as mybir
from concourse.masks import make_identity

K, H, N, T, S, T2, M = 1024, 512, 768, 4096, 1024, 2048, 1024
FLOPS = 2 * (2 * K * H * S + H * N * M)

F32 = mybir.dt.float32
BF16 = mybir.dt.bfloat16
I32 = mybir.dt.int32
U32 = mybir.dt.uint32
U16 = mybir.dt.uint16
U8 = mybir.dt.uint8
FP8X4 = mybir.dt.float8_e4m3fn_x4
FP4X4 = mybir.dt.float4_e2m1fn_x4
ACT = mybir.ActivationFunctionType
ALU = mybir.AluOpType

P = 128
K_PASS = 512
HALF = 512
PER_COLUMN = 16
TWO_PI = 2.0 * math.pi
VECTOR_UNITS = 2
SHARED_BANKS = 4
W3_STEP = 256
CHUNKS = [256, 256, 256, 128, 128]


def tile_list_frog_chorus_phase_kernel(
    tc, tab_words, tab_scales, offs, wa, wp_words, wp_scales, phase0, lift, wgs, offs2, wgt, offs3, rain, w3, out
):
    nc = tc.nc
    with ExitStack() as ctx:
        keep = ctx.enter_context(tc.tile_pool(name="keep", bufs=1))
        work = ctx.enter_context(tc.tile_pool(name="work", bufs=3))
        psum = ctx.enter_context(tc.psum_pool(name="psum", bufs=1))

        pick = keep.tile([P, S // PER_COLUMN], U16, name="pick")
        put = keep.tile([P, S // PER_COLUMN], U16, name="put")
        read = keep.tile([P, M // PER_COLUMN], U16, name="read")
        phase0_sb = keep.tile([P, 4], F32, name="phase0_sb")
        lift_sb = keep.tile([P, 4], F32, name="lift_sb")
        tab_sc = keep.tile([P, T], U8, name="tab_sc", align_bytes=64)
        wp_raw = [
            keep.tile([P, 2 * H], U8, name="wp_raw0", tag="slot_b", align_bytes=64),
            keep.tile([P, 2 * H], U8, name="wp_raw1", tag="slot_c", align_bytes=64),
        ]
        picked_sc = keep.tile([P, S], U8, name="picked_sc", align_bytes=64)
        tab0 = keep.tile([P, T], U32, name="tab0", tag="slot_e", align_bytes=64)
        wp_sc_raw = keep.tile([P, 2, H], U8, name="wp_sc_raw", align_bytes=64)
        v_sc = [keep.tile([P, S], U8, name="v_sc%d" % a, align_bytes=64) for a in range(2)]

        def load_words(tile, a):
            nc.sync.dma_start(tile[:].bitcast(I32), tab_words[a].rearrange("p t i -> p (t i)").bitcast(I32))

        def load_wa(tile, a):
            nc.sync.dma_start(tile[:], wa[a * K_PASS : (a + 1) * K_PASS, :].rearrange("(p j) c -> p j c", j=4))

        nc.sync.dma_start(tab_sc[0:32, :].bitcast(I32), tab_scales.rearrange("a q t -> (a q) t").bitcast(I32))
        nc.sync.dma_start(pick[:], offs)
        for a in range(2):
            nc.sync.dma_start(wp_raw[a][:].bitcast(I32), wp_words[a].bitcast(I32))
        nc.sync.dma_start(phase0_sb[:], phase0.rearrange("(p t) -> p t", t=4))
        nc.sync.dma_start(lift_sb[:], lift.rearrange("(p t) -> p t", t=4))
        nc.sync.dma_start(put[:], offs2)
        load_words(tab0, 0)
        nc.sync.dma_start(read[:], offs3)
        tab1 = keep.tile([P, T], U32, name="tab1", tag="slot_a", align_bytes=64)
        load_words(tab1, 1)

        nc.vector.memset(wp_sc_raw[:].bitcast(I32), 0)
        nc.vector.memset(tab_sc[32:64, :].bitcast(I32), 0)
        nc.vector.memset(tab_sc[64:128, :].bitcast(I32), 0)
        for a in range(2):
            nc.vector.memset(v_sc[a][:].bitcast(I32), 0)
        for q in range(4):
            nc.gpsimd.dma_start(
                wp_sc_raw[32 * q : 32 * q + 4, :, :].bitcast(I32),
                wp_scales[:, 4 * q : 4 * q + 4, :].rearrange("a r c -> r a c").bitcast(I32),
            )

        identity = keep.tile([P, P], F32, name="identity", align_bytes=64)
        make_identity(nc, identity[:])

        nc.vector.tensor_copy(picked_sc[:], tab_sc[:].indirect(pick[:]))
        moves = [(a, q) for a in range(2) for q in range(4)][1:]
        for a, q in moves:
            queue = nc.gpsimd if (a, q) == moves[-1] else nc.sync
            row = 16 * a + 4 * q
            queue.dma_start(v_sc[a][32 * q : 32 * q + 4, :].bitcast(I32), picked_sc[row : row + 4, :].bitcast(I32))
        nc.vector.tensor_copy(v_sc[0][0:4, :].bitcast(I32), picked_sc[0:4, :].bitcast(I32))
        tab = [tab0, tab1]

        wp = keep.tile([P, 2, 4, 2 * P], U8, name="wp", align_bytes=64)
        wp_sc = keep.tile([P, 2, 4, P], U8, name="wp_sc", align_bytes=64)
        for a in range(2):
            nc.vector.tensor_copy(
                wp[:, a].bitcast(U16),
                wp_raw[a][:].bitcast(U16).rearrange("p (m t) -> p t m", t=4),
            )
        wa_raw = [
            keep.tile([P, 4, H], F32, name="wa_raw0", tag="slot_b", align_bytes=64),
            keep.tile([P, 4, H], F32, name="wa_raw1", tag="slot_c", align_bytes=64),
        ]
        load_wa(wa_raw[0], 0)
        load_wa(wa_raw[1], 1)

        page0 = keep.tile([P, T2], F32, name="page0", align_bytes=64)
        nc.vector.memset(page0[:], 0.0)

        v = [[keep.tile([P, HALF], U32, name="v%d_%d" % (a, h), align_bytes=64) for h in range(2)] for a in range(2)]

        def entries(j0, j1):
            return slice(j0 // PER_COLUMN, j1 // PER_COLUMN)

        def gather_words(a, h):
            nc.vector.tensor_copy(v[a][h][:], tab[a][:].indirect(pick[:, entries(h * HALF, (h + 1) * HALF)]))

        gather_words(0, 0)
        gather_words(0, 1)
        page1 = keep.tile([P, T2], F32, name="page1", tag="slot_e", align_bytes=64)
        nc.vector.memset(page1[:], 0.0)
        pages = [page0, page1]

        nc.vector.tensor_copy(wp_sc[:], wp_sc_raw[:].rearrange("p a (m t) -> p a t m", t=4))
        cos_bias = keep.tile([P, 4], F32, name="cos_bias")
        lift_bias = keep.tile([P, 4], F32, name="lift_bias")
        nc.vector.tensor_scalar_add(cos_bias[:], phase0_sb[:], -0.5 * math.pi)
        nc.vector.tensor_tensor(lift_bias[:], phase0_sb[:], lift_sb[:], ALU.mult)

        gather_words(1, 0)
        gather_words(1, 1)
        wgs_sb = keep.tile([P, S], F32, name="wgs_sb", tag="slot_a", align_bytes=64)
        for h in range(2):
            nc.sync.dma_start(wgs_sb[:, h * HALF : (h + 1) * HALF], wgs[:, h * HALF : (h + 1) * HALF])

        lifted, sines, gated, hs = {}, {}, {}, {}
        wa_codes, wa_sc = {}, {}

        def shared_bank(i):
            return "bank%d" % (i % SHARED_BANKS)

        def phase_terms(u):
            t, h = divmod(u, 2)
            acc = psum.tile([P, HALF], F32, name="acc_p", tag="acc_p", bufs=2)
            for a in range(2):
                nc.tensor.matmul_mx(
                    out=acc[:],
                    lhsT=wp[:, a, t, :].bitcast(FP4X4),
                    lhsT_scale=wp_sc[:, a, t, :],
                    rhs=v[a][h][:].bitcast(FP8X4),
                    rhs_scale=v_sc[a][:, h * HALF : (h + 1) * HALF],
                    start=(a == 0),
                    stop=(a == 1),
                )
            folded = work.tile([P, HALF], F32, name="folded", tag="folded")
            count = work.tile([P, HALF], U32, name="count", tag="count", bufs=2)
            size = work.tile([P, HALF], F32, name="size", tag="size", bufs=2)
            if h == 0:
                lifted[t] = work.tile([P, S], F32, name="lifted", tag="lifted")
            sines[u] = work.tile([P, HALF], F32, name="sine", tag="sine", bufs=4)

            def lift_phase():
                nc.scalar.activation(
                    lifted[t][:, h * HALF : (h + 1) * HALF],
                    acc[:],
                    ACT.Identity,
                    bias=lift_bias[:, t : t + 1],
                    scale=lift_sb[:, t : t + 1],
                )

            nc.scalar.activation(folded[:], acc[:], ACT.Abs, bias=cos_bias[:, t : t + 1])
            nc.scalar.activation(count[:], folded[:], ACT.Copy, scale=1.0 / TWO_PI)
            if u < VECTOR_UNITS:
                rest = work.tile([P, HALF], F32, name="rest", tag="turns")
                nc.vector.scalar_tensor_tensor(rest[:], count[:].bitcast(I32), -TWO_PI, folded[:], ALU.mult, ALU.add)
                nc.scalar.activation(size[:], rest[:], ACT.Abs)
                nc.scalar.activation(sines[u][:], size[:], ACT.Sin, bias=0.5 * math.pi, scale=-1.0)
                lift_phase()
            else:
                turns = work.tile([P, HALF], F32, name="turns", tag="turns")
                nc.scalar.activation(turns[:], count[:], ACT.Copy, scale=-TWO_PI)
                lift_phase()
                rest_t = psum.tile([P, HALF], F32, name="rest_t", tag="rest_t", bufs=2)
                for j0 in range(0, HALF, P):
                    cols = slice(j0, j0 + P)
                    for term, first in ((folded, True), (turns, False)):
                        nc.tensor.matmul(
                            rest_t[:, cols], term[:, cols], identity[:], start=first, stop=not first, is_transpose=True
                        )
                sine_t = work.tile([P, HALF], F32, name="sine_t", tag="sine_t", bufs=2)
                nc.scalar.activation(size[:], rest_t[:], ACT.Abs)
                nc.scalar.activation(sine_t[:], size[:], ACT.Sin, bias=0.5 * math.pi, scale=-1.0)
                back = psum.tile([P, HALF], F32, name="back", tag=shared_bank(u))
                for j0 in range(0, HALF, P):
                    nc.tensor.transpose(back[:, j0 : j0 + P], sine_t[:, j0 : j0 + P], identity[:])
                nc.scalar.copy(sines[u][:], back[:])

        def quantise_wa(a, t0, t1):
            n = t1 - t0
            label = "%d_%d" % (a, t0)
            rounded = keep.tile([P, n, P, 4], BF16, name="wa_bf" + label, tag="wa_bf" + label, align_bytes=64)
            codes = keep.tile([P, n, P], U32, name="wa_codes" + label, align_bytes=64)
            scales = keep.tile([P, n, P], U8, name="wa_sc" + label, align_bytes=64)
            nc.vector.tensor_copy(
                rounded[:].rearrange("p t m j -> p m j t"),
                wa_raw[a][:].rearrange("p j (m t) -> p m j t", t=4)[:, :, :, t0:t1],
            )
            nc.vector.quantize_mx(
                out=codes[:].rearrange("p t m -> p (t m)").bitcast(FP8X4),
                scales=scales[:].rearrange("p t m -> p (t m)"),
                in_=rounded[:].rearrange("p t m j -> p (t m j)"),
            )
            for t in range(t0, t1):
                wa_codes[a, t] = codes[:, t - t0, :]
                wa_sc[a, t] = scales[:, t - t0, :]

        def loud(u):
            t, h = divmod(u, 2)
            acc = psum.tile([P, HALF], F32, name="acc_l", tag=shared_bank(u))
            for a in range(2):
                nc.tensor.matmul_mx(
                    out=acc[:],
                    lhsT=wa_codes[a, t].bitcast(FP8X4),
                    lhsT_scale=wa_sc[a, t],
                    rhs=v[a][h][:].bitcast(FP8X4),
                    rhs_scale=v_sc[a][:, h * HALF : (h + 1) * HALF],
                    start=(a == 0),
                    stop=(a == 1),
                )
            if h == 0:
                gated[t] = work.tile([P, S], F32, name="gated", tag="gated", bufs=2)
            nc.vector.tensor_tensor(gated[t][:, h * HALF : (h + 1) * HALF], acc[:], sines[u][:], ALU.mult)

        def combine(t, j0, j1):
            if j0 == 0:
                hs[t] = work.tile([P, S], F32, name="h", tag="h", bufs=2)
            nc.vector.tensor_tensor(hs[t][:, j0:j1], gated[t][:, j0:j1], lifted[t][:, j0:j1], ALU.add)

        def scatter(t, j0, j1):
            nc.vector.tensor_tensor(
                pages[t % 2][:].indirect(put[:, entries(j0, j1)]), hs[t][:, j0:j1], wgs_sb[:, j0:j1], ALU.mult
            )

        def unit_columns(u):
            t, h = divmod(u, 2)
            return t, h * HALF, (h + 1) * HALF

        x = keep.tile([P, 4, M], F32, name="x", align_bytes=64)

        def gather(t, m0, m1):
            nc.vector.tensor_tensor(
                x[:, t, m0:m1], pages[t % 2][:].indirect(read[:, entries(m0, m1)]), wgt_sb[:, m0:m1], ALU.mult
            )

        w3_bf = keep.tile([P, N, 4], BF16, name="w3_bf", align_bytes=64)
        w3_codes = keep.tile([P, N], U32, name="w3_codes", align_bytes=64)
        w3_sc = keep.tile([P, N], U8, name="w3_sc", align_bytes=64)

        def quantise_w3(n0, n1):
            nc.scalar.copy(
                w3_bf[:, n0:n1, :].rearrange("p (c i) j -> p c j i", i=4),
                w3_raw[:, :, n0:n1].rearrange("p j (c i) -> p c j i", i=4),
            )
            nc.vector.quantize_mx(
                out=w3_codes[:, n0:n1].bitcast(FP8X4),
                scales=w3_sc[:, n0:n1],
                in_=w3_bf[:, n0:n1, :].rearrange("p n j -> p (n j)"),
            )

        phase_terms(0)
        quantise_wa(0, 0, 4)
        wgt_sb = keep.tile([P, M], F32, name="wgt_sb", tag="wa_bf0_0", align_bytes=64)
        rain_sb = keep.tile([P, 4, M], F32, name="rain_sb", tag="slot_b", align_bytes=64)
        nc.sync.dma_start(wgt_sb[:], wgt)
        nc.sync.dma_start(rain_sb[:], rain.rearrange("(p j) m -> p j m", j=4))
        quantise_wa(1, 0, 1)
        phase_terms(1)
        loud(0)
        combine(*unit_columns(0))
        quantise_wa(1, 1, 2)
        quantise_wa(1, 2, 4)
        w3_raw = keep.tile([P, 4, N], F32, name="w3_raw", tag="slot_c", align_bytes=64)
        nc.sync.dma_start(w3_raw[:], w3.rearrange("(p j) n -> p j n", j=4))

        for u in range(4):
            phase_terms(u + 2)
            loud(u + 1)
            scatter(*unit_columns(u))
            if u + 1 < 4:
                combine(*unit_columns(u + 1))
            if u + 1 == 3:
                gather(0, 0, M)

        phase_terms(6)
        loud(5)
        phase_terms(7)
        gather(1, 0, M)
        combine(2, 0, S)
        loud(6)
        scatter(2, 0, S)
        loud(7)
        for n0 in range(0, N, W3_STEP):
            quantise_w3(n0, n0 + W3_STEP)
        combine(3, 0, S)
        gather(2, 0, CHUNKS[0])
        scatter(3, 0, S)

        out_v = out.rearrange("(c p) m -> p c m", p=P)
        edges = [sum(CHUNKS[:c]) for c in range(len(CHUNKS) + 1)]
        last = len(CHUNKS) - 1

        def add_rain(m0, m1):
            z = work.tile([P, m1 - m0, 4], BF16, name="z", tag="z", align_bytes=64)
            nc.vector.tensor_tensor(
                z[:].rearrange("p (c i) t -> p c t i", i=4),
                x[:, :, m0:m1].rearrange("p t (c i) -> p c t i", i=4),
                rain_sb[:, :, m0:m1].rearrange("p t (c i) -> p c t i", i=4),
                ALU.add,
            )
            return z

        def finish(c, z):
            m0, m1 = edges[c], edges[c + 1]
            w = m1 - m0
            codes = work.tile([P, w], U32, name="z_codes", tag="z_codes", align_bytes=64)
            scales = work.tile([P, w], U8, name="z_sc", tag="z_sc", align_bytes=64)
            nc.vector.quantize_mx(out=codes[:].bitcast(FP8X4), scales=scales[:], in_=z[:].rearrange("p m t -> p (m t)"))
            per_bank = 2 if w == CHUNKS[0] else 3
            for b in range(N // P // per_bank):
                acc = psum.tile([P, per_bank, w], F32, name="acc_o", tag=shared_bank(3 * c + b))
                for i in range(per_bank):
                    n0 = (per_bank * b + i) * P
                    nc.tensor.matmul_mx(
                        out=acc[:, i, :],
                        lhsT=w3_codes[:, n0 : n0 + P].bitcast(FP8X4),
                        lhsT_scale=w3_sc[:, n0 : n0 + P],
                        rhs=codes[:].bitcast(FP8X4),
                        rhs_scale=scales[:],
                        start=True,
                        stop=True,
                    )
                res = work.tile([P, per_bank, w], F32, name="res", tag="res", bufs=8)
                if c == last and b == 1:
                    nc.vector.tensor_copy(res[:], acc[:])
                else:
                    nc.scalar.copy(res[:], acc[:])
                nc.sync.dma_start(out_v[:, per_bank * b : per_bank * (b + 1), m0:m1], res[:])

        gather(3, edges[0], edges[1])
        for c in range(len(CHUNKS)):
            if c < last:
                gather(2, edges[c + 1], edges[c + 2])
            z = add_rain(edges[c], edges[c + 1])
            if c < last:
                gather(3, edges[c + 1], edges[c + 2])
            finish(c, z)
